import numpy as np
import ml_dtypes


def mxq(x, axis, fmt="e4m3"):
    dtype, down = {"e4m3": (ml_dtypes.float8_e4m3fn, 7), "e5m2": (ml_dtypes.float8_e5m2, 14)}[fmt]
    v = np.moveaxis(np.asarray(x, np.float32).astype(ml_dtypes.bfloat16).astype(np.float64), axis, -1)
    blocks = v.reshape(v.shape[:-1] + (-1, 32))
    amax = np.abs(blocks).max(-1, keepdims=True)
    byte = np.maximum(np.where(amax > 0, np.frexp(amax)[1] - 1 + 127, 0) - down, 1)
    scale = np.exp2(byte - 127.0)
    codes = (blocks / scale).astype(np.float32).astype(dtype).astype(np.float64)
    return np.moveaxis((codes * scale).reshape(v.shape), -1, axis)


WIDE = False


def mx_kscale(k):
    if not WIDE:
        return np.ones(k)
    levels = np.array([10, -10, 5, -5, 0])
    if k % 512:
        return np.exp2(np.random.permutation(np.resize(levels, k // 32))).repeat(32)
    a = np.empty((k // 512, 16))
    for p in range(k // 512):
        a[p, :8] = np.random.permutation(np.resize(levels, 8))
        for g in range(8):
            far = levels[np.abs(levels - a[p, g]) >= 10]
            a[p, g + 8] = far[np.random.randint(len(far))]
    return np.exp2(a.ravel()).repeat(32)


def f64(x):
    return np.asarray(x).astype(np.float64)


def striped(idx):
    return np.tile(np.asarray(idx).reshape(-1, 16).T, (8, 1)).astype(np.uint16)


def unstriped(offs):
    return offs[:16].T.reshape(-1).astype(np.int64)


def striped8(idx):
    return np.asarray(idx).reshape(8, -1, 16).transpose(0, 2, 1).reshape(128, -1).astype(np.uint16)


def unstriped8(offs):
    return offs.reshape(8, 16, -1).transpose(0, 2, 1).reshape(8, -1).astype(np.int64)


def pick8(x, idx, run):
    r = np.arange(len(x))
    return x[r[:, None], idx[r % (8 * run) // run]]


E2M1 = np.array([0.0, 0.5, 1.0, 1.5, 2.0, 3.0, 4.0, 6.0, -0.0, -0.5, -1.0, -1.5, -2.0, -3.0, -4.0, -6.0])


def pack_weight(w, fmt):
    k, n = w.shape
    w = f64(np.asarray(w, np.float32).astype(ml_dtypes.bfloat16)).reshape(k // 32, 32, n)
    amax = np.abs(w).max(1)
    if fmt == "e4m3":
        byte = np.frexp(amax)[1] - 1 + 127 - 7
    else:
        mant, ex = np.frexp(amax / 6.0)
        byte = np.where(mant > 0.5, ex, ex - 1) + 127
    byte = np.clip(np.where(amax > 0, byte, 1), 1, 254)
    scaled = (w * np.exp2(127.0 - byte)[:, None, :]).reshape(k, n).astype(np.float32)
    by_word = np.ascontiguousarray(scaled.reshape(k // 512, 128, 4, n).transpose(0, 1, 3, 2))
    if fmt == "e4m3":
        words = by_word.astype(ml_dtypes.float8_e4m3fn).view(np.uint8)
    else:
        c = by_word.astype(ml_dtypes.float4_e2m1fn).view(np.uint8) & 0xF
        words = (c[..., 0::2] | (c[..., 1::2] << 4)).reshape(k // 512, 128, 2 * n)
    return np.ascontiguousarray(words), np.ascontiguousarray(byte.astype(np.uint8).reshape(k // 512, 16, n))


def unpack_weight(words, scales, fmt):
    g, _, n = scales.shape
    words = np.ascontiguousarray(words).reshape(g, 128, n, -1)
    if fmt == "e4m3":
        vals = words.view(ml_dtypes.float8_e4m3fn).astype(np.float64)
    else:
        nib = np.empty((g, 128, n, 4), np.uint8)
        nib[..., 0::2] = words & 0xF
        nib[..., 1::2] = words >> 4
        vals = E2M1[nib]
    vals = vals * np.repeat(np.exp2(scales.astype(np.float64) - 127.0), 8, axis=1)[..., None]
    return vals.transpose(0, 1, 3, 2).reshape(g * 512, n)


K, J, R, T, F, G, O, N, U, E = 512, 512, 512, 2048, 2048, 1024, 256, 256, 128, 512


def setup_inputs():
    n = np.random.standard_normal
    idx = np.random.permutation(T)[:J]
    idx2 = np.stack([np.random.permutation(F)[:G] for _ in range(8)])
    idx3 = np.random.permutation(G)[:R]
    idx4 = np.stack([np.random.permutation(J)[:O] for _ in range(8)])
    idx5 = np.random.permutation(E)[:O]
    idx6 = np.stack([np.random.permutation(E)[:U] for _ in range(8)])
    idx7 = np.stack([np.random.permutation(O)[:U] for _ in range(8)])
    fk = mx_kscale(K)
    fr = mx_kscale(R)
    xtp = pack_weight(n((K, T)) * fk[:, None], "e4m3")
    wbp = pack_weight(n((R, N)) * 1 / np.sqrt(R) / fr[:, None], "e4m3")
    wop = pack_weight(n((R, N)) * 1 / np.sqrt(R) / fr[:, None], "e2m1")
    return {
        "xt_words": xtp[0],
        "xt_scales": xtp[1],
        "ua": (np.random.randint(-7, 8, (K, F)).astype(np.float64)).astype(np.float32),
        "ha": ((np.random.randint(8, 25, (K, 1)) / 1024.0) / fk[:, None]).astype(np.float32),
        "hb": (np.random.uniform(0.5, 1.6, (K, 1))).astype(np.float32),
        "sa": (np.random.uniform(0.5, 1.6, (R, 1)) * fr[:, None]).astype(np.float32),
        "wb_words": wbp[0],
        "wb_scales": wbp[1],
        "wo_words": wop[0],
        "wo_scales": wop[1],
        "so": (np.random.uniform(0.5, 1.6, (N, 1))).astype(np.float32),
        "sp": (np.random.uniform(0.5, 1.6, (N, 1))).astype(np.float32),
        "offs": striped(idx),
        "offs2": striped8(idx2),
        "offs3": striped(idx3),
        "offs4": striped8(idx4),
        "offs5": striped(idx5),
        "offs6": striped8(idx6),
        "offs7": striped8(idx7),
    }


def reference(xt_words, xt_scales, ua, ha, hb, sa, wb_words, wb_scales, wo_words, wo_scales, so, sp, offs, offs2, offs3, offs4, offs5, offs6, offs7):
    idx = unstriped(offs)
    idx2 = unstriped8(offs2)
    idx3 = unstriped(offs3)
    idx4 = unstriped8(offs4)
    idx5 = unstriped(offs5)
    idx6 = unstriped8(offs6)
    idx7 = unstriped8(offs7)
    xtu = unpack_weight(xt_words, xt_scales, "e4m3")
    wbu = unpack_weight(wb_words, wb_scales, "e4m3")
    wou = unpack_weight(wo_words, wo_scales, "e2m1")
    wcd = pick8(f64(ua), idx2, 64) * f64(ha)
    wc = wcd[:, idx3] * f64(hb)
    wcq = mxq(wc, 0, "e4m3")
    xtidxg = xtu[:, idx]
    a = wcq.T @ xtidxg
    g1 = np.maximum(a, 0.0)
    hid = pick8(g1, idx4, 64) * f64(sa)
    hidq = mxq(hid, 0, "e4m3")
    p = wbu.T @ hidq
    q = wou.T @ hidq
    m0 = np.zeros((N, E))
    m0[:, idx5] = p
    y = np.maximum(pick8(m0, idx6, 16) * f64(so), pick8(q, idx7, 16) * f64(sp))
    return y

@@ -1,0 +1,235 @@
+from contextlib import ExitStack
+
+import concourse.mybir as mybir
+
+K, J, R, T, F, G, O, N, U, E = 512, 512, 512, 2048, 2048, 1024, 256, 256, 128, 512
+FLOPS = 2 * K * R * J + 2 * 2 * R * N * O
+
+F32 = mybir.dt.float32
+BF16 = mybir.dt.bfloat16
+I32 = mybir.dt.int32
+U32 = mybir.dt.uint32
+U16 = mybir.dt.uint16
+U8 = mybir.dt.uint8
+FP8X4 = mybir.dt.float8_e4m3fn_x4
+FP4X4 = mybir.dt.float4_e2m1fn_x4
+ACT = mybir.ActivationFunctionType
+ALU = mybir.AluOpType
+
+P = 128
+PACK = 4
+LANES = 16
+HALVES = 2
+
+
+def tile_picked_tokens_respelled_one_kept_outcomes_outboard_kernel(
+    tc, xt_words, xt_scales, ua, ha, hb, sa, wb_words, wb_scales, wo_words, wo_scales, so, sp,
+    offs, offs2, offs3, offs4, offs5, offs6, offs7, out,
+):
+    nc = tc.nc
+    with ExitStack() as ctx:
+        keep = ctx.enter_context(tc.tile_pool(name="keep", bufs=1))
+        psum = ctx.enter_context(tc.psum_pool(name="psum", bufs=8))
+
+        def sb(name, width, dtype):
+            return keep.tile([P, width], dtype, name=name, align_bytes=64)
+
+        def load_list(name, source):
+            tile = keep.tile(list(source.shape), U16, name=name)
+            nc.sync.dma_start(tile[:], source)
+            return tile
+
+        def load_by_word(engine, name, source):
+            tile = sb(name, PACK, F32)
+            engine.dma_start(tile[:], source.rearrange("(p t) o -> p (t o)", t=PACK))
+            return tile
+
+        def load_by_block(name, source):
+            tile = sb(name, N // P, F32)
+            with nc.allow_non_contiguous_dma(reason="one value a partition for each block of 128 rows"):
+                nc.sync.dma_start(tile[:], source.rearrange("(c p) o -> p (c o)", p=P))
+            return tile
+
+        def load_scales(name, source, width):
+            staged = sb(name + "_staged", width, I32)
+            nc.sync.dma_start(
+                staged[0:4, :].rearrange("r (q c) -> r q c", q=4),
+                source[0].bitcast(I32).rearrange("(q r) c -> r q c", r=4),
+            )
+            return staged
+
+        def spread_scales(name, staged, width):
+            tile = sb(name, width, U8)
+            nc.vector.memset(tile[:].bitcast(I32), 0)
+            words = width // 4
+            for quad in range(4):
+                nc.vector.tensor_copy(
+                    tile[32 * quad : 32 * quad + 4, :].bitcast(I32), staged[0:4, quad * words : (quad + 1) * words]
+                )
+            return tile
+
+        def entries(tile, start, count):
+            return tile[:, start // LANES : (start + count) // LANES]
+
+        ua_rows = ua.rearrange("(p t) f -> t p f", t=PACK)
+        ua_sb = [sb("ua%d" % t, F, F32) for t in range(PACK)]
+        list2 = load_list("list2", offs2)
+        ha_sb = load_by_word(nc.scalar, "ha_sb", ha)
+        nc.sync.dma_start(ua_sb[0][:], ua_rows[0])
+        hb_sb = load_by_word(nc.scalar, "hb_sb", hb)
+        list3 = load_list("list3", offs3)
+        nc.sync.dma_start(ua_sb[1][:], ua_rows[1])
+        xs_staged = load_scales("xs", xt_scales, T)
+        list1 = load_list("list1", offs)
+        xw_sb = sb("xw_sb", T, U32)
+        nc.sync.dma_start(xw_sb[:].bitcast(I32), xt_words[0].rearrange("p n t -> p (n t)").bitcast(I32))
+        nc.sync.dma_start(ua_sb[2][:], ua_rows[2])
+        nc.sync.dma_start(ua_sb[3][:], ua_rows[3])
+        list4 = load_list("list4", offs4)
+        sa_sb = load_by_word(nc.sync, "sa_sb", sa)
+        wbs_staged = load_scales("wbs", wb_scales, N)
+        wos_staged = load_scales("wos", wo_scales, N)
+        wbw_sb = sb("wbw_sb", N, U32)
+        nc.sync.dma_start(wbw_sb[:].bitcast(I32), wb_words[0].rearrange("p n t -> p (n t)").bitcast(I32))
+        wow_sb = sb("wow_sb", 2 * N, U8)
+        nc.sync.dma_start(wow_sb[:].bitcast(I32), wo_words[0].bitcast(I32))
+        list5 = load_list("list5", offs5)
+        list6 = load_list("list6", offs6)
+        list7 = load_list("list7", offs7)
+        so_sb = load_by_block("so_sb", so)
+        sp_sb = load_by_block("sp_sb", sp)
+        xs_sb = spread_scales("xs_sb", xs_staged, T)
+        wbs_sb = spread_scales("wbs_sb", wbs_staged, N)
+        wos_sb = spread_scales("wos_sb", wos_staged, N)
+
+        boards = []
+        for c in range(N // P):
+            board = sb("board%d" % c, E, F32)
+            nc.vector.memset(board[:], 0.0)
+            boards.append(board)
+
+        xw_got = sb("xw_got", J, U32)
+        xs_got = sb("xs_got", J, U8)
+        nc.vector.tensor_copy(xs_got[:], xs_sb[:].indirect(list1[:]))
+        nc.vector.tensor_copy(xw_got[:], xw_sb[:].indirect(list1[:]))
+
+        wc_in = sb("wc_in", PACK * R, BF16)
+        wc_view = wc_in[:].rearrange("p (s m t) -> p m s t", s=PACK, t=PACK)
+        for t in range(PACK):
+            wcd = sb("wcd%d" % t, G, F32)
+            nc.scalar.activation(wcd[:], ua_sb[t][:].indirect(list2[:]), ACT.Copy, scale=ha_sb[:, t : t + 1])
+            pieces = HALVES if t == PACK - 1 else 1
+            size = R // pieces
+            for h in range(pieces):
+                wc = sb("wc%d_%d" % (t, h), size, BF16)
+                nc.scalar.activation(
+                    wc[:], wcd[:].indirect(entries(list3, h * size, size)), ACT.Copy, scale=hb_sb[:, t : t + 1]
+                )
+                src = wc[:].rearrange("p (m s) -> p m s", s=PACK)
+                m0 = h * size // PACK
+                m1 = m0 + size // PACK
+                if h == 0:
+                    nc.vector.tensor_copy(wc_view[:, m0:m1, :, t], src)
+                else:
+                    for s0 in range(0, PACK, 2):
+                        nc.vector.tensor_copy(wc_view[:, m0:m1, s0 : s0 + 2, t], src[:, :, s0 : s0 + 2])
+
+        wc_words, wc_scales = [], []
+        for s in range(PACK):
+            words = sb("wc_words%d" % s, P, U32)
+            scales = sb("wc_scales%d" % s, P, U8)
+            nc.vector.quantize_mx(
+                out=words[:].bitcast(FP8X4), scales=scales[:], in_=wc_in[:, s * PACK * P : (s + 1) * PACK * P]
+            )
+            wc_words.append(words)
+            wc_scales.append(scales)
+
+        half_j = J // HALVES
+        half_o = O // HALVES
+        hid_in = [sb("hid_in%d" % h, PACK * half_o, BF16) for h in range(HALVES)]
+        hid_view = [tile[:].rearrange("p (o s) -> p o s", s=PACK) for tile in hid_in]
+        early = sb("hid_early", (PACK - 1) * O, BF16)
+        early_view = early[:].rearrange("p (s o) -> p o s", s=PACK - 1)
+        late = []
+        for s in range(PACK):
+            g1 = sb("g1_%d" % s, J, F32)
+            for h in range(HALVES):
+                cols = slice(h * half_j, (h + 1) * half_j)
+                acc = psum.tile([P, half_j], F32, name="acc")
+                nc.tensor.matmul_mx(
+                    out=acc[:], lhsT=wc_words[s][:].bitcast(FP8X4), lhsT_scale=wc_scales[s][:],
+                    rhs=xw_got[:, cols].bitcast(FP8X4), rhs_scale=xs_got[:, cols], start=True, stop=True,
+                )
+                if s == 0 and h == 1:
+                    nc.scalar.activation(g1[:, cols], acc[:], ACT.Relu)
+                else:
+                    nc.vector.tensor_scalar_max(g1[:, cols], acc[:], 0.0)
+            if s < PACK - 1:
+                nc.scalar.activation(
+                    early[:, s * O : (s + 1) * O], g1[:].indirect(list4[:]), ACT.Copy, scale=sa_sb[:, s : s + 1]
+                )
+            else:
+                for h in range(HALVES):
+                    piece = sb("hid_late%d" % h, half_o, BF16)
+                    nc.scalar.activation(
+                        piece[:], g1[:].indirect(entries(list4, h * half_o, half_o)), ACT.Copy,
+                        scale=sa_sb[:, s : s + 1],
+                    )
+                    late.append(piece)
+
+        hid_words = sb("hid_words", O, U32)
+        hid_scales = sb("hid_scales", O, U8)
+        for h in range(HALVES):
+            nc.vector.tensor_copy(hid_view[h][:, :, 0 : PACK - 1], early_view[:, h * half_o : (h + 1) * half_o, :])
+        for h in range(HALVES):
+            cols = slice(h * half_o, (h + 1) * half_o)
+            nc.vector.tensor_copy(hid_view[h][:, :, PACK - 1], late[h][:])
+            nc.vector.quantize_mx(out=hid_words[:, cols].bitcast(FP8X4), scales=hid_scales[:, cols], in_=hid_in[h][:])
+
+        p_acc = {}
+        for h in range(HALVES):
+            cols = slice(h * half_o, (h + 1) * half_o)
+            for c in (1, 0):
+                acc = psum.tile([P, half_j], F32, name="acc")
+                nc.tensor.matmul_mx(
+                    out=acc[:, 0:half_o], lhsT=wbw_sb[:, c * P : (c + 1) * P].bitcast(FP8X4),
+                    lhsT_scale=wbs_sb[:, c * P : (c + 1) * P],
+                    rhs=hid_words[:, cols].bitcast(FP8X4), rhs_scale=hid_scales[:, cols], start=True, stop=True,
+                )
+                p_acc[(c, h)] = acc
+        q_acc = []
+        for c in range(N // P):
+            acc = psum.tile([P, half_j], F32, name="acc")
+            nc.tensor.matmul_mx(
+                out=acc[:], lhsT=wow_sb[:, 2 * c * P : 2 * (c + 1) * P].bitcast(FP4X4),
+                lhsT_scale=wos_sb[:, c * P : (c + 1) * P],
+                rhs=hid_words[:].bitcast(FP8X4), rhs_scale=hid_scales[:], start=True, stop=True,
+            )
+            q_acc.append(acc)
+
+        p0 = sb("p0", O, F32)
+        p1 = [sb("p1_%d" % h, half_o, F32) for h in range(HALVES)]
+        nc.scalar.copy(p1[0][:], p_acc[(1, 0)][:, 0:half_o])
+        nc.vector.tensor_copy(p0[:, 0:half_o], p_acc[(0, 0)][:, 0:half_o])
+        nc.vector.tensor_copy(p1[1][:], p_acc[(1, 1)][:, 0:half_o])
+        nc.vector.tensor_copy(p0[:, half_o:O], p_acc[(0, 1)][:, 0:half_o])
+        q_sb = []
+        for c in range(N // P):
+            tile = sb("q%d" % c, O, F32)
+            nc.vector.tensor_copy(tile[:], q_acc[c][:])
+            q_sb.append(tile)
+        for h in range(HALVES):
+            nc.scalar.activation(boards[1][:].indirect(entries(list5, h * half_o, half_o)), p1[h][:], ACT.Copy)
+        nc.vector.tensor_copy(boards[0][:].indirect(list5[:]), p0[:])
+
+        second = []
+        for c in (1, 0):
+            tile = sb("second%d" % c, U, F32)
+            nc.scalar.activation(tile[:], q_sb[c][:].indirect(list7[:]), ACT.Copy, scale=sp_sb[:, c : c + 1])
+            second.append(tile)
+        for i, c in enumerate((1, 0)):
+            first = sb("first%d" % c, U, F32)
+            nc.scalar.activation(first[:], boards[c][:].indirect(list6[:]), ACT.Copy, scale=so_sb[:, c : c + 1])
+            larger = sb("larger%d" % c, U, F32)
+            nc.vector.tensor_tensor(larger[:], first[:], second[i][:], ALU.max)
+            nc.sync.dma_start(out[c * P : (c + 1) * P, :], larger[:])

@@ -71,6 +71,11 @@ def tile_picked_tokens_respelled_one_kept_outcomes_outboard_kernel(
         def entries(tile, start, count):
             return tile[:, start // LANES : (start + count) // LANES]
 
+        warm_in = sb("warm_in", 1, F32)
+        warm_out = sb("warm_out", 1, F32)
+        nc.vector.memset(warm_in[:], 0.0)
+        nc.scalar.activation(warm_out[:], warm_in[:], ACT.Copy)
+
         ua_rows = ua.rearrange("(p t) f -> t p f", t=PACK)
         ua_sb = [sb("ua%d" % t, F, F32) for t in range(PACK)]
         list2 = load_list("list2", offs2)

@@ -31,8 +31,8 @@ def tile_picked_tokens_respelled_one_kept_outcomes_outboard_kernel(
         keep = ctx.enter_context(tc.tile_pool(name="keep", bufs=1))
         psum = ctx.enter_context(tc.psum_pool(name="psum", bufs=8))
 
-        def sb(name, width, dtype):
-            return keep.tile([P, width], dtype, name=name, align_bytes=64)
+        def sb(name, width, dtype, tag=None):
+            return keep.tile([P, width], dtype, name=name, tag=tag or name, align_bytes=64)
 
         def load_list(name, source):
             tile = keep.tile(list(source.shape), U16, name=name)
@@ -86,10 +86,10 @@ def tile_picked_tokens_respelled_one_kept_outcomes_outboard_kernel(
         nc.sync.dma_start(ua_sb[1][:], ua_rows[1])
         xs_staged = load_scales("xs", xt_scales, T)
         list1 = load_list("list1", offs)
-        xw_sb = sb("xw_sb", T, U32)
-        nc.sync.dma_start(xw_sb[:].bitcast(I32), xt_words[0].rearrange("p n t -> p (n t)").bitcast(I32))
         nc.sync.dma_start(ua_sb[2][:], ua_rows[2])
         nc.sync.dma_start(ua_sb[3][:], ua_rows[3])
+        xw_sb = sb("xw_sb", T, U32, tag="tokens")
+        nc.sync.dma_start(xw_sb[:].bitcast(I32), xt_words[0].rearrange("p n t -> p (n t)").bitcast(I32))
         list4 = load_list("list4", offs4)
         sa_sb = load_by_word(nc.sync, "sa_sb", sa)
         wbs_staged = load_scales("wbs", wb_scales, N)
@@ -125,22 +125,20 @@ def tile_picked_tokens_respelled_one_kept_outcomes_outboard_kernel(
             nc.scalar.activation(wcd[:], ua_sb[t][:].indirect(list2[:]), ACT.Copy, scale=ha_sb[:, t : t + 1])
             pieces = HALVES if t == PACK - 1 else 1
             size = R // pieces
+            wc = sb("wc%d" % t, R, BF16, tag="tokens" if t == PACK - 1 else None)
             for h in range(pieces):
-                wc = sb("wc%d_%d" % (t, h), size, BF16)
                 nc.scalar.activation(
-                    wc[:], wcd[:].indirect(entries(list3, h * size, size)), ACT.Copy, scale=hb_sb[:, t : t + 1]
+                    wc[:, h * size : (h + 1) * size], wcd[:].indirect(entries(list3, h * size, size)), ACT.Copy, scale=hb_sb[:, t : t + 1]
                 )
-                src = wc[:].rearrange("p (m s) -> p m s", s=PACK)
+                src = wc[:, h * size : (h + 1) * size].rearrange("p (m s) -> p m s", s=PACK)
                 m0 = h * size // PACK
                 m1 = m0 + size // PACK
                 if h == 0:
                     nc.vector.tensor_copy(wc_view[:, m0:m1, :, t], src)
-                else:
-                    for s0 in range(0, PACK, 2):
-                        nc.vector.tensor_copy(wc_view[:, m0:m1, s0 : s0 + 2, t], src[:, :, s0 : s0 + 2])
 
         wc_words, wc_scales = [], []
         for s in range(PACK):
+            nc.vector.tensor_copy(wc_view[:, m0:m1, s, PACK - 1], src[:, :, s])
             words = sb("wc_words%d" % s, P, U32)
             scales = sb("wc_scales%d" % s, P, U8)
             nc.vector.quantize_mx(
@@ -153,11 +151,20 @@ def tile_picked_tokens_respelled_one_kept_outcomes_outboard_kernel(
         half_o = O // HALVES
         hid_in = [sb("hid_in%d" % h, PACK * half_o, BF16) for h in range(HALVES)]
         hid_view = [tile[:].rearrange("p (o s) -> p o s", s=PACK) for tile in hid_in]
-        early = sb("hid_early", (PACK - 1) * O, BF16)
-        early_view = early[:].rearrange("p (s o) -> p o s", s=PACK - 1)
-        late = []
+        hid_low = sb("hid_low", 2 * O, BF16)
+        hid_high = {}
+        g1_sb = []
+
+        def fetch_half(s, h, tag=None):
+            tile = sb("hid%d_%d" % (s, h), half_o, BF16, tag=tag)
+            nc.scalar.activation(
+                tile[:], g1_sb[s][:].indirect(entries(list4, h * half_o, half_o)), ACT.Copy, scale=sa_sb[:, s : s + 1]
+            )
+            hid_high[(s, h)] = tile
+
         for s in range(PACK):
             g1 = sb("g1_%d" % s, J, F32)
+            g1_sb.append(g1)
             for h in range(HALVES):
                 cols = slice(h * half_j, (h + 1) * half_j)
                 acc = psum.tile([P, half_j], F32, name="acc")
@@ -165,30 +172,28 @@ def tile_picked_tokens_respelled_one_kept_outcomes_outboard_kernel(
                     out=acc[:], lhsT=wc_words[s][:].bitcast(FP8X4), lhsT_scale=wc_scales[s][:],
                     rhs=xw_got[:, cols].bitcast(FP8X4), rhs_scale=xs_got[:, cols], start=True, stop=True,
                 )
-                if s == 0 and h == 1:
+                if s == 0:
                     nc.scalar.activation(g1[:, cols], acc[:], ACT.Relu)
                 else:
                     nc.vector.tensor_scalar_max(g1[:, cols], acc[:], 0.0)
-            if s < PACK - 1:
+            if s < 2:
                 nc.scalar.activation(
-                    early[:, s * O : (s + 1) * O], g1[:].indirect(list4[:]), ACT.Copy, scale=sa_sb[:, s : s + 1]
+                    hid_low[:, s * O : (s + 1) * O], g1[:].indirect(list4[:]), ACT.Copy, scale=sa_sb[:, s : s + 1]
                 )
             else:
-                for h in range(HALVES):
-                    piece = sb("hid_late%d" % h, half_o, BF16)
-                    nc.scalar.activation(
-                        piece[:], g1[:].indirect(entries(list4, h * half_o, half_o)), ACT.Copy,
-                        scale=sa_sb[:, s : s + 1],
-                    )
-                    late.append(piece)
+                fetch_half(s, 0)
+        fetch_half(3, 1)
+        fetch_half(2, 1, tag="g1_3")
 
         hid_words = sb("hid_words", O, U32)
         hid_scales = sb("hid_scales", O, U8)
+        low_view = hid_low[:].rearrange("p (s o) -> p o s", s=2)
         for h in range(HALVES):
-            nc.vector.tensor_copy(hid_view[h][:, :, 0 : PACK - 1], early_view[:, h * half_o : (h + 1) * half_o, :])
-        for h in range(HALVES):
+            nc.vector.tensor_copy(hid_view[h][:, :, 0:2], low_view[:, h * half_o : (h + 1) * half_o, :])
+        for h, planes in ((0, (2, 3)), (1, (3, 2))):
             cols = slice(h * half_o, (h + 1) * half_o)
-            nc.vector.tensor_copy(hid_view[h][:, :, PACK - 1], late[h][:])
+            for s in planes:
+                nc.vector.tensor_copy(hid_view[h][:, :, s], hid_high[(s, h)][:])
             nc.vector.quantize_mx(out=hid_words[:, cols].bitcast(FP8X4), scales=hid_scales[:, cols], in_=hid_in[h][:])
 
         p_acc = {}
@@ -202,39 +207,45 @@ def tile_picked_tokens_respelled_one_kept_outcomes_outboard_kernel(
                     rhs=hid_words[:, cols].bitcast(FP8X4), rhs_scale=hid_scales[:, cols], start=True, stop=True,
                 )
                 p_acc[(c, h)] = acc
-        q_acc = []
-        for c in range(N // P):
+        q_acc = {}
+        for c in (1, 0):
             acc = psum.tile([P, half_j], F32, name="acc")
             nc.tensor.matmul_mx(
                 out=acc[:], lhsT=wow_sb[:, 2 * c * P : 2 * (c + 1) * P].bitcast(FP4X4),
                 lhsT_scale=wos_sb[:, c * P : (c + 1) * P],
                 rhs=hid_words[:].bitcast(FP8X4), rhs_scale=hid_scales[:], start=True, stop=True,
             )
-            q_acc.append(acc)
+            q_acc[c] = acc
 
-        p0 = sb("p0", O, F32)
-        p1 = [sb("p1_%d" % h, half_o, F32) for h in range(HALVES)]
-        nc.scalar.copy(p1[0][:], p_acc[(1, 0)][:, 0:half_o])
-        nc.vector.tensor_copy(p0[:, 0:half_o], p_acc[(0, 0)][:, 0:half_o])
-        nc.vector.tensor_copy(p1[1][:], p_acc[(1, 1)][:, 0:half_o])
-        nc.vector.tensor_copy(p0[:, half_o:O], p_acc[(0, 1)][:, 0:half_o])
-        q_sb = []
-        for c in range(N // P):
-            tile = sb("q%d" % c, O, F32)
-            nc.vector.tensor_copy(tile[:], q_acc[c][:])
-            q_sb.append(tile)
+        q_sb = {}
         for h in range(HALVES):
-            nc.scalar.activation(boards[1][:].indirect(entries(list5, h * half_o, half_o)), p1[h][:], ACT.Copy)
-        nc.vector.tensor_copy(boards[0][:].indirect(list5[:]), p0[:])
+            picks = entries(list5, h * half_o, half_o)
+            p1 = sb("p1_%d" % h, half_o, F32)
+            nc.scalar.copy(p1[:], p_acc[(1, h)][:, 0:half_o])
+            nc.scalar.activation(boards[1][:].indirect(picks), p1[:], ACT.Copy)
+            p0 = sb("p0_%d" % h, half_o, F32)
+            nc.vector.tensor_copy(p0[:], p_acc[(0, h)][:, 0:half_o])
+            if h == HALVES - 1:
+                for c in (1, 0):
+                    q_sb[c] = sb("q%d" % c, O, F32)
+                    nc.vector.tensor_copy(q_sb[c][:], q_acc[c][:])
+            nc.vector.tensor_copy(boards[0][:].indirect(picks), p0[:])
 
-        second = []
-        for c in (1, 0):
+        def from_board(c):
+            tile = sb("first%d" % c, U, F32)
+            nc.scalar.activation(tile[:], boards[c][:].indirect(list6[:]), ACT.Copy, scale=so_sb[:, c : c + 1])
+            return tile
+
+        def from_q(c):
             tile = sb("second%d" % c, U, F32)
             nc.scalar.activation(tile[:], q_sb[c][:].indirect(list7[:]), ACT.Copy, scale=sp_sb[:, c : c + 1])
-            second.append(tile)
-        for i, c in enumerate((1, 0)):
-            first = sb("first%d" % c, U, F32)
-            nc.scalar.activation(first[:], boards[c][:].indirect(list6[:]), ACT.Copy, scale=so_sb[:, c : c + 1])
+            return tile
+
+        def store_larger(c, first, second):
             larger = sb("larger%d" % c, U, F32)
-            nc.vector.tensor_tensor(larger[:], first[:], second[i][:], ALU.max)
+            nc.vector.tensor_tensor(larger[:], first[:], second[:], ALU.max)
             nc.sync.dma_start(out[c * P : (c + 1) * P, :], larger[:])
+
+        for c in (1, 0):
+            second = from_q(c)
+            store_larger(c, from_board(c), second)

@@ -44,6 +44,11 @@ def tile_picked_tokens_respelled_one_kept_outcomes_outboard_kernel(
             engine.dma_start(tile[:], source.rearrange("(p t) o -> p (t o)", t=PACK))
             return tile
 
+        def load_pair(name, source, first):
+            tile = sb(name, 2, F32)
+            nc.sync.dma_start(tile[:], source.rearrange("(p t) o -> p (t o)", t=PACK)[:, first : first + 2])
+            return tile
+
         def load_by_block(name, source):
             tile = sb(name, N // P, F32)
             with nc.allow_non_contiguous_dma(reason="one value a partition for each block of 128 rows"):
@@ -81,15 +86,16 @@ def tile_picked_tokens_respelled_one_kept_outcomes_outboard_kernel(
         list2 = load_list("list2", offs2)
         ha_sb = load_by_word(nc.scalar, "ha_sb", ha)
         nc.sync.dma_start(ua_sb[0][:], ua_rows[0])
-        hb_sb = load_by_word(nc.scalar, "hb_sb", hb)
-        list3 = load_list("list3", offs3)
         nc.sync.dma_start(ua_sb[1][:], ua_rows[1])
+        nc.sync.dma_start(ua_sb[2][:], ua_rows[2])
         xs_staged = load_scales("xs", xt_scales, T)
         list1 = load_list("list1", offs)
-        nc.sync.dma_start(ua_sb[2][:], ua_rows[2])
+        list3 = load_list("list3", offs3)
+        hb_pairs = [load_pair("hb_low", hb, 0)]
         nc.sync.dma_start(ua_sb[3][:], ua_rows[3])
-        xw_sb = sb("xw_sb", T, U32, tag="tokens")
+        xw_sb = sb("xw_sb", T, U32)
         nc.sync.dma_start(xw_sb[:].bitcast(I32), xt_words[0].rearrange("p n t -> p (n t)").bitcast(I32))
+        hb_pairs.append(load_pair("hb_high", hb, 2))
         list4 = load_list("list4", offs4)
         sa_sb = load_by_word(nc.sync, "sa_sb", sa)
         wbs_staged = load_scales("wbs", wb_scales, N)
@@ -125,10 +131,10 @@ def tile_picked_tokens_respelled_one_kept_outcomes_outboard_kernel(
             nc.scalar.activation(wcd[:], ua_sb[t][:].indirect(list2[:]), ACT.Copy, scale=ha_sb[:, t : t + 1])
             pieces = HALVES if t == PACK - 1 else 1
             size = R // pieces
-            wc = sb("wc%d" % t, R, BF16, tag="tokens" if t == PACK - 1 else None)
+            wc = sb("wc%d" % t, R, BF16)
             for h in range(pieces):
                 nc.scalar.activation(
-                    wc[:, h * size : (h + 1) * size], wcd[:].indirect(entries(list3, h * size, size)), ACT.Copy, scale=hb_sb[:, t : t + 1]
+                    wc[:, h * size : (h + 1) * size], wcd[:].indirect(entries(list3, h * size, size)), ACT.Copy, scale=hb_pairs[t // 2][:, t % 2 : t % 2 + 1]
                 )
                 src = wc[:, h * size : (h + 1) * size].rearrange("p (m s) -> p m s", s=PACK)
                 m0 = h * size // PACK

@@ -44,10 +44,11 @@ def tile_picked_tokens_respelled_one_kept_outcomes_outboard_kernel(
             engine.dma_start(tile[:], source.rearrange("(p t) o -> p (t o)", t=PACK))
             return tile
 
-        def load_pair(name, source, first):
-            tile = sb(name, 2, F32)
-            nc.sync.dma_start(tile[:], source.rearrange("(p t) o -> p (t o)", t=PACK)[:, first : first + 2])
-            return tile
+        def load_columns(name, source, first, count):
+            tile = sb(name, count, F32)
+            with nc.allow_non_contiguous_dma(reason="one or two values a partition"):
+                nc.sync.dma_start(tile[:], source.rearrange("(p t) o -> p (t o)", t=PACK)[:, first : first + count])
+            return [tile[:, i : i + 1] for i in range(count)]
 
         def load_by_block(name, source):
             tile = sb(name, N // P, F32)
@@ -55,21 +56,27 @@ def tile_picked_tokens_respelled_one_kept_outcomes_outboard_kernel(
                 nc.sync.dma_start(tile[:], source.rearrange("(c p) o -> p (c o)", p=P))
             return tile
 
-        def load_scales(name, source, width):
-            staged = sb(name + "_staged", width, I32)
-            nc.sync.dma_start(
-                staged[0:4, :].rearrange("r (q c) -> r q c", q=4),
-                source[0].bitcast(I32).rearrange("(q r) c -> r q c", r=4),
-            )
+        def load_scales(name, source, width, groups):
+            quads = 4 // groups
+            staged = sb(name + "_staged", quads * width // 4, I32)
+            rows = source[0].bitcast(I32)
+            for group in range(groups):
+                nc.sync.dma_start(
+                    staged[64 * group : 64 * group + 4, :].rearrange("r (q c) -> r q c", q=quads),
+                    rows[4 * quads * group : 4 * quads * (group + 1), :].rearrange("(q r) c -> r q c", r=4),
+                )
             return staged
 
-        def spread_scales(name, staged, width):
+        def spread_scales(name, staged, width, groups):
+            quads = 4 // groups
             tile = sb(name, width, U8)
             nc.vector.memset(tile[:].bitcast(I32), 0)
             words = width // 4
             for quad in range(4):
+                row = 64 * (quad // quads)
+                col = words * (quad % quads)
                 nc.vector.tensor_copy(
-                    tile[32 * quad : 32 * quad + 4, :].bitcast(I32), staged[0:4, quad * words : (quad + 1) * words]
+                    tile[32 * quad : 32 * quad + 4, :].bitcast(I32), staged[row : row + 4, col : col + words]
                 )
             return tile
 
@@ -83,23 +90,24 @@ def tile_picked_tokens_respelled_one_kept_outcomes_outboard_kernel(
 
         ua_rows = ua.rearrange("(p t) f -> t p f", t=PACK)
         ua_sb = [sb("ua%d" % t, F, F32) for t in range(PACK)]
+        nc.sync.dma_start(ua_sb[0][:], ua_rows[0])
         list2 = load_list("list2", offs2)
         ha_sb = load_by_word(nc.scalar, "ha_sb", ha)
-        nc.sync.dma_start(ua_sb[0][:], ua_rows[0])
+        list3 = load_list("list3", offs3)
+        hb_cols = load_columns("hb0", hb, 0, 1)
         nc.sync.dma_start(ua_sb[1][:], ua_rows[1])
         nc.sync.dma_start(ua_sb[2][:], ua_rows[2])
-        xs_staged = load_scales("xs", xt_scales, T)
+        xs_staged = load_scales("xs", xt_scales, T, 2)
         list1 = load_list("list1", offs)
-        list3 = load_list("list3", offs3)
-        hb_pairs = [load_pair("hb_low", hb, 0)]
+        hb_cols = hb_cols + load_columns("hb1", hb, 1, 1)
+        wbs_staged = load_scales("wbs", wb_scales, N, 1)
+        wos_staged = load_scales("wos", wo_scales, N, 1)
         nc.sync.dma_start(ua_sb[3][:], ua_rows[3])
         xw_sb = sb("xw_sb", T, U32)
         nc.sync.dma_start(xw_sb[:].bitcast(I32), xt_words[0].rearrange("p n t -> p (n t)").bitcast(I32))
-        hb_pairs.append(load_pair("hb_high", hb, 2))
+        hb_cols = hb_cols + load_columns("hb2", hb, 2, 2)
         list4 = load_list("list4", offs4)
         sa_sb = load_by_word(nc.sync, "sa_sb", sa)
-        wbs_staged = load_scales("wbs", wb_scales, N)
-        wos_staged = load_scales("wos", wo_scales, N)
         wbw_sb = sb("wbw_sb", N, U32)
         nc.sync.dma_start(wbw_sb[:].bitcast(I32), wb_words[0].rearrange("p n t -> p (n t)").bitcast(I32))
         wow_sb = sb("wow_sb", 2 * N, U8)
@@ -109,9 +117,9 @@ def tile_picked_tokens_respelled_one_kept_outcomes_outboard_kernel(
         list7 = load_list("list7", offs7)
         so_sb = load_by_block("so_sb", so)
         sp_sb = load_by_block("sp_sb", sp)
-        xs_sb = spread_scales("xs_sb", xs_staged, T)
-        wbs_sb = spread_scales("wbs_sb", wbs_staged, N)
-        wos_sb = spread_scales("wos_sb", wos_staged, N)
+        xs_sb = spread_scales("xs_sb", xs_staged, T, 2)
+        wbs_sb = spread_scales("wbs_sb", wbs_staged, N, 1)
+        wos_sb = spread_scales("wos_sb", wos_staged, N, 1)
 
         boards = []
         for c in range(N // P):
@@ -134,7 +142,7 @@ def tile_picked_tokens_respelled_one_kept_outcomes_outboard_kernel(
             wc = sb("wc%d" % t, R, BF16)
             for h in range(pieces):
                 nc.scalar.activation(
-                    wc[:, h * size : (h + 1) * size], wcd[:].indirect(entries(list3, h * size, size)), ACT.Copy, scale=hb_pairs[t // 2][:, t % 2 : t % 2 + 1]
+                    wc[:, h * size : (h + 1) * size], wcd[:].indirect(entries(list3, h * size, size)), ACT.Copy, scale=hb_cols[t]
                 )
                 src = wc[:, h * size : (h + 1) * size].rearrange("p (m s) -> p m s", s=PACK)
                 m0 = h * size // PACK

from contextlib import ExitStack

import concourse.mybir as mybir

K, J, R, T, F, G, O, N, U, E = 512, 512, 512, 2048, 2048, 1024, 256, 256, 128, 512
FLOPS = 2 * K * R * J + 2 * 2 * R * N * O

F32 = mybir.dt.float32
BF16 = mybir.dt.bfloat16
I32 = mybir.dt.int32
U32 = mybir.dt.uint32
U16 = mybir.dt.uint16
U8 = mybir.dt.uint8
FP8X4 = mybir.dt.float8_e4m3fn_x4
FP4X4 = mybir.dt.float4_e2m1fn_x4
ACT = mybir.ActivationFunctionType
ALU = mybir.AluOpType

P = 128
PACK = 4
LANES = 16
HALVES = 2


def tile_picked_tokens_respelled_one_kept_outcomes_outboard_kernel(
    tc, xt_words, xt_scales, ua, ha, hb, sa, wb_words, wb_scales, wo_words, wo_scales, so, sp,
    offs, offs2, offs3, offs4, offs5, offs6, offs7, out,
):
    nc = tc.nc
    with ExitStack() as ctx:
        keep = ctx.enter_context(tc.tile_pool(name="keep", bufs=1))
        psum = ctx.enter_context(tc.psum_pool(name="psum", bufs=8))

        def sb(name, width, dtype, tag=None):
            return keep.tile([P, width], dtype, name=name, tag=tag or name, align_bytes=64)

        def load_list(name, source):
            tile = keep.tile(list(source.shape), U16, name=name)
            nc.sync.dma_start(tile[:], source)
            return tile

        def load_by_word(engine, name, source):
            tile = sb(name, PACK, F32)
            engine.dma_start(tile[:], source.rearrange("(p t) o -> p (t o)", t=PACK))
            return tile

        def load_columns(name, source, first, count):
            tile = sb(name, count, F32)
            with nc.allow_non_contiguous_dma(reason="one or two values a partition"):
                nc.sync.dma_start(tile[:], source.rearrange("(p t) o -> p (t o)", t=PACK)[:, first : first + count])
            return [tile[:, i : i + 1] for i in range(count)]

        def load_by_block(name, source):
            tile = sb(name, N // P, F32)
            with nc.allow_non_contiguous_dma(reason="one value a partition for each block of 128 rows"):
                nc.sync.dma_start(tile[:], source.rearrange("(c p) o -> p (c o)", p=P))
            return tile

        def load_scales(name, source, width, groups):
            quads = 4 // groups
            staged = sb(name + "_staged", quads * width // 4, I32)
            rows = source[0].bitcast(I32)
            for group in range(groups):
                nc.sync.dma_start(
                    staged[64 * group : 64 * group + 4, :].rearrange("r (q c) -> r q c", q=quads),
                    rows[4 * quads * group : 4 * quads * (group + 1), :].rearrange("(q r) c -> r q c", r=4),
                )
            return staged

        def spread_scales(name, staged, width, groups):
            quads = 4 // groups
            tile = sb(name, width, U8)
            nc.vector.memset(tile[:].bitcast(I32), 0)
            words = width // 4
            for quad in range(4):
                row = 64 * (quad // quads)
                col = words * (quad % quads)
                nc.vector.tensor_copy(
                    tile[32 * quad : 32 * quad + 4, :].bitcast(I32), staged[row : row + 4, col : col + words]
                )
            return tile

        def entries(tile, start, count):
            return tile[:, start // LANES : (start + count) // LANES]

        warm_in = sb("warm_in", 1, F32)
        warm_out = sb("warm_out", 1, F32)
        nc.vector.memset(warm_in[:], 0.0)
        nc.scalar.activation(warm_out[:], warm_in[:], ACT.Copy)

        ua_rows = ua.rearrange("(p t) f -> t p f", t=PACK)
        ua_sb = [sb("ua%d" % t, F, F32) for t in range(PACK)]
        nc.sync.dma_start(ua_sb[0][:], ua_rows[0])
        list2 = load_list("list2", offs2)
        ha_sb = load_by_word(nc.scalar, "ha_sb", ha)
        list3 = load_list("list3", offs3)
        hb_cols = load_columns("hb0", hb, 0, 1)
        nc.sync.dma_start(ua_sb[1][:], ua_rows[1])
        nc.sync.dma_start(ua_sb[2][:], ua_rows[2])
        xs_staged = load_scales("xs", xt_scales, T, 2)
        list1 = load_list("list1", offs)
        hb_cols = hb_cols + load_columns("hb1", hb, 1, 1)
        wbs_staged = load_scales("wbs", wb_scales, N, 1)
        wos_staged = load_scales("wos", wo_scales, N, 1)
        nc.sync.dma_start(ua_sb[3][:], ua_rows[3])
        xw_sb = sb("xw_sb", T, U32)
        nc.sync.dma_start(xw_sb[:].bitcast(I32), xt_words[0].rearrange("p n t -> p (n t)").bitcast(I32))
        hb_cols = hb_cols + load_columns("hb2", hb, 2, 2)
        list4 = load_list("list4", offs4)
        sa_sb = load_by_word(nc.sync, "sa_sb", sa)
        wbw_sb = sb("wbw_sb", N, U32)
        nc.sync.dma_start(wbw_sb[:].bitcast(I32), wb_words[0].rearrange("p n t -> p (n t)").bitcast(I32))
        wow_sb = sb("wow_sb", 2 * N, U8)
        nc.sync.dma_start(wow_sb[:].bitcast(I32), wo_words[0].bitcast(I32))
        list5 = load_list("list5", offs5)
        list6 = load_list("list6", offs6)
        list7 = load_list("list7", offs7)
        so_sb = load_by_block("so_sb", so)
        sp_sb = load_by_block("sp_sb", sp)
        xs_sb = spread_scales("xs_sb", xs_staged, T, 2)
        wbs_sb = spread_scales("wbs_sb", wbs_staged, N, 1)
        wos_sb = spread_scales("wos_sb", wos_staged, N, 1)

        boards = []
        for c in range(N // P):
            board = sb("board%d" % c, E, F32)
            nc.vector.memset(board[:], 0.0)
            boards.append(board)

        xw_got = sb("xw_got", J, U32)
        xs_got = sb("xs_got", J, U8)
        nc.vector.tensor_copy(xs_got[:], xs_sb[:].indirect(list1[:]))
        nc.vector.tensor_copy(xw_got[:], xw_sb[:].indirect(list1[:]))

        wc_in = sb("wc_in", PACK * R, BF16)
        wc_view = wc_in[:].rearrange("p (s m t) -> p m s t", s=PACK, t=PACK)
        for t in range(PACK):
            wcd = sb("wcd%d" % t, G, F32)
            nc.scalar.activation(wcd[:], ua_sb[t][:].indirect(list2[:]), ACT.Copy, scale=ha_sb[:, t : t + 1])
            pieces = HALVES if t == PACK - 1 else 1
            size = R // pieces
            wc = sb("wc%d" % t, R, BF16)
            for h in range(pieces):
                nc.scalar.activation(
                    wc[:, h * size : (h + 1) * size], wcd[:].indirect(entries(list3, h * size, size)), ACT.Copy, scale=hb_cols[t]
                )
                src = wc[:, h * size : (h + 1) * size].rearrange("p (m s) -> p m s", s=PACK)
                m0 = h * size // PACK
                m1 = m0 + size // PACK
                if h == 0:
                    nc.vector.tensor_copy(wc_view[:, m0:m1, :, t], src)

        wc_words, wc_scales = [], []
        for s in range(PACK):
            nc.vector.tensor_copy(wc_view[:, m0:m1, s, PACK - 1], src[:, :, s])
            words = sb("wc_words%d" % s, P, U32)
            scales = sb("wc_scales%d" % s, P, U8)
            nc.vector.quantize_mx(
                out=words[:].bitcast(FP8X4), scales=scales[:], in_=wc_in[:, s * PACK * P : (s + 1) * PACK * P]
            )
            wc_words.append(words)
            wc_scales.append(scales)

        half_j = J // HALVES
        half_o = O // HALVES
        hid_in = [sb("hid_in%d" % h, PACK * half_o, BF16) for h in range(HALVES)]
        hid_view = [tile[:].rearrange("p (o s) -> p o s", s=PACK) for tile in hid_in]
        hid_low = sb("hid_low", 2 * O, BF16)
        hid_high = {}
        g1_sb = []

        def fetch_half(s, h, tag=None):
            tile = sb("hid%d_%d" % (s, h), half_o, BF16, tag=tag)
            nc.scalar.activation(
                tile[:], g1_sb[s][:].indirect(entries(list4, h * half_o, half_o)), ACT.Copy, scale=sa_sb[:, s : s + 1]
            )
            hid_high[(s, h)] = tile

        for s in range(PACK):
            g1 = sb("g1_%d" % s, J, F32)
            g1_sb.append(g1)
            for h in range(HALVES):
                cols = slice(h * half_j, (h + 1) * half_j)
                acc = psum.tile([P, half_j], F32, name="acc")
                nc.tensor.matmul_mx(
                    out=acc[:], lhsT=wc_words[s][:].bitcast(FP8X4), lhsT_scale=wc_scales[s][:],
                    rhs=xw_got[:, cols].bitcast(FP8X4), rhs_scale=xs_got[:, cols], start=True, stop=True,
                )
                if s == 0:
                    nc.scalar.activation(g1[:, cols], acc[:], ACT.Relu)
                else:
                    nc.vector.tensor_scalar_max(g1[:, cols], acc[:], 0.0)
            if s < 2:
                nc.scalar.activation(
                    hid_low[:, s * O : (s + 1) * O], g1[:].indirect(list4[:]), ACT.Copy, scale=sa_sb[:, s : s + 1]
                )
            else:
                fetch_half(s, 0)
        fetch_half(3, 1)
        fetch_half(2, 1, tag="g1_3")

        hid_words = sb("hid_words", O, U32)
        hid_scales = sb("hid_scales", O, U8)
        low_view = hid_low[:].rearrange("p (s o) -> p o s", s=2)
        for h in range(HALVES):
            nc.vector.tensor_copy(hid_view[h][:, :, 0:2], low_view[:, h * half_o : (h + 1) * half_o, :])
        for h, planes in ((0, (2, 3)), (1, (3, 2))):
            cols = slice(h * half_o, (h + 1) * half_o)
            for s in planes:
                nc.vector.tensor_copy(hid_view[h][:, :, s], hid_high[(s, h)][:])
            nc.vector.quantize_mx(out=hid_words[:, cols].bitcast(FP8X4), scales=hid_scales[:, cols], in_=hid_in[h][:])

        p_acc = {}
        for h in range(HALVES):
            cols = slice(h * half_o, (h + 1) * half_o)
            for c in (1, 0):
                acc = psum.tile([P, half_j], F32, name="acc")
                nc.tensor.matmul_mx(
                    out=acc[:, 0:half_o], lhsT=wbw_sb[:, c * P : (c + 1) * P].bitcast(FP8X4),
                    lhsT_scale=wbs_sb[:, c * P : (c + 1) * P],
                    rhs=hid_words[:, cols].bitcast(FP8X4), rhs_scale=hid_scales[:, cols], start=True, stop=True,
                )
                p_acc[(c, h)] = acc
        q_acc = {}
        for c in (1, 0):
            acc = psum.tile([P, half_j], F32, name="acc")
            nc.tensor.matmul_mx(
                out=acc[:], lhsT=wow_sb[:, 2 * c * P : 2 * (c + 1) * P].bitcast(FP4X4),
                lhsT_scale=wos_sb[:, c * P : (c + 1) * P],
                rhs=hid_words[:].bitcast(FP8X4), rhs_scale=hid_scales[:], start=True, stop=True,
            )
            q_acc[c] = acc

        q_sb = {}
        for h in range(HALVES):
            picks = entries(list5, h * half_o, half_o)
            p1 = sb("p1_%d" % h, half_o, F32)
            nc.scalar.copy(p1[:], p_acc[(1, h)][:, 0:half_o])
            nc.scalar.activation(boards[1][:].indirect(picks), p1[:], ACT.Copy)
            p0 = sb("p0_%d" % h, half_o, F32)
            nc.vector.tensor_copy(p0[:], p_acc[(0, h)][:, 0:half_o])
            if h == HALVES - 1:
                for c in (1, 0):
                    q_sb[c] = sb("q%d" % c, O, F32)
                    nc.vector.tensor_copy(q_sb[c][:], q_acc[c][:])
            nc.vector.tensor_copy(boards[0][:].indirect(picks), p0[:])

        def from_board(c):
            tile = sb("first%d" % c, U, F32)
            nc.scalar.activation(tile[:], boards[c][:].indirect(list6[:]), ACT.Copy, scale=so_sb[:, c : c + 1])
            return tile

        def from_q(c):
            tile = sb("second%d" % c, U, F32)
            nc.scalar.activation(tile[:], q_sb[c][:].indirect(list7[:]), ACT.Copy, scale=sp_sb[:, c : c + 1])
            return tile

        def store_larger(c, first, second):
            larger = sb("larger%d" % c, U, F32)
            nc.vector.tensor_tensor(larger[:], first[:], second[:], ALU.max)
            nc.sync.dma_start(out[c * P : (c + 1) * P, :], larger[:])

        for c in (1, 0):
            second = from_q(c)
            store_larger(c, from_board(c), second)
